import numpy as np
import ml_dtypes


def mxq(x, axis, fmt="e4m3"):
    dtype, down = {"e4m3": (ml_dtypes.float8_e4m3fn, 7), "e5m2": (ml_dtypes.float8_e5m2, 14)}[fmt]
    v = np.moveaxis(np.asarray(x, np.float32).astype(ml_dtypes.bfloat16).astype(np.float64), axis, -1)
    blocks = v.reshape(v.shape[:-1] + (-1, 32))
    amax = np.abs(blocks).max(-1, keepdims=True)
    byte = np.maximum(np.where(amax > 0, np.frexp(amax)[1] - 1 + 127, 0) - down, 1)
    scale = np.exp2(byte - 127.0)
    codes = (blocks / scale).astype(np.float32).astype(dtype).astype(np.float64)
    return np.moveaxis((codes * scale).reshape(v.shape), -1, axis)


WIDE = False


def mx_kscale(k):
    if not WIDE:
        return np.ones(k)
    levels = np.array([10, -10, 5, -5, 0])
    if k % 512:
        return np.exp2(np.random.permutation(np.resize(levels, k // 32))).repeat(32)
    a = np.empty((k // 512, 16))
    for p in range(k // 512):
        a[p, :8] = np.random.permutation(np.resize(levels, 8))
        for g in range(8):
            far = levels[np.abs(levels - a[p, g]) >= 10]
            a[p, g + 8] = far[np.random.randint(len(far))]
    return np.exp2(a.ravel()).repeat(32)


def f64(x):
    return np.asarray(x).astype(np.float64)


def striped(idx):
    return np.tile(idx.reshape(-1, 16).T, (8, 1)).astype(np.uint16)


def unstriped(offs):
    return offs[:16].T.reshape(-1).astype(np.int64)


def silu(v):
    return v / (1.0 + np.exp(-np.maximum(v, -700.0)))


K, T, S, N = 1536, 1024, 512, 128


def setup_inputs():
    n = np.random.standard_normal
    s = mx_kscale(K)[:, None]
    return {
        "xT": (n((K, S)) * s).astype(np.float32),
        "w": (n((K, N)) / np.sqrt(K) / s).astype(np.float32),
        "b": (0.3 * n((N, 1))).astype(np.float32),
        "gate": np.tile(np.random.uniform(0.2, 1.0, S), (N, 1)).astype(np.float32),
        "offs": striped(np.sort(np.random.permutation(T)[:S])),
    }


def reference(xT, w, b, gate, offs):
    idx = unstriped(offs)
    xq = mxq(f64(xT), 0, "e4m3")
    y = mxq(f64(w), 0, "e4m3").T @ xq
    y = silu(y + f64(b))
    out = np.zeros((N, T))
    out[:, idx] = f64(gate) * y
    return out

@@ -1,0 +1,115 @@
+from contextlib import ExitStack
+
+import concourse.mybir as mybir
+
+K, S, M, T = 1536, 512, 128, 1024
+FLOPS = 2 * K * S * M
+
+F32 = mybir.dt.float32
+BF16 = mybir.dt.bfloat16
+U32 = mybir.dt.uint32
+U16 = mybir.dt.uint16
+U8 = mybir.dt.uint8
+FP8X4 = mybir.dt.float8_e4m3fn_x4
+SILU = mybir.ActivationFunctionType.Silu
+MULT = mybir.AluOpType.mult
+
+P = 128
+J = 4
+PASSES = K // (P * J)
+H = S // 2
+
+
+def interleave(copy, dst, src):
+    copy(
+        out=dst.rearrange("p (c i) j -> p c j i", i=4),
+        in_=src.rearrange("p j (c i) -> p c j i", i=4),
+    )
+
+
+def quantize(nc, codes, scales, grouped):
+    nc.vector.quantize_mx(
+        out=codes.bitcast(FP8X4),
+        scales=scales,
+        in_=grouped.rearrange("p n j -> p (n j)"),
+    )
+
+
+def tile_picked_place_lin_silu_srt_l_kernel(tc, xT, w, b, gate, offs, out):
+    nc = tc.nc
+    with ExitStack() as ctx:
+        keep = ctx.enter_context(tc.tile_pool(name="keep", bufs=1))
+        psum = ctx.enter_context(tc.psum_pool(name="psum", bufs=1))
+
+        offs_sb = keep.tile([P, S // 16], U16, name="offs_sb")
+        b_sb = keep.tile([P, 1], F32, name="b_sb")
+        gate_sb = keep.tile([P, S], F32, name="gate_sb")
+        window = keep.tile([P, T], F32, name="window")
+        y = keep.tile([P, S], F32, name="y")
+        warm = keep.tile([P, 1], F32, name="warm")
+
+        w_raw = keep.tile([P, PASSES, J, M], F32, name="w_raw")
+        w_grp = keep.tile([P, PASSES, M, J], BF16, name="w_grp", align_bytes=64)
+        w_codes = keep.tile([P, PASSES, M], U32, name="w_codes", align_bytes=64)
+        w_scales = keep.tile([P, PASSES, M], U8, name="w_scales", align_bytes=64)
+        x_raw = [keep.tile([P, J, S], F32, name=f"x_raw{c}") for c in range(PASSES - 1)]
+        x_half = [keep.tile([P, J, H], F32, name=f"x_half{h}") for h in range(2)]
+        x_grp = [keep.tile([P, S, J], BF16, name=f"x_grp{c}", align_bytes=64) for c in range(PASSES)]
+        x_codes = [keep.tile([P, S], U32, name=f"x_codes{c}", align_bytes=64) for c in range(PASSES)]
+        x_scales = [keep.tile([P, S], U8, name=f"x_scales{c}", align_bytes=64) for c in range(PASSES)]
+        acc = [psum.tile([M, H], F32, name=f"acc{h}") for h in range(2)]
+
+        x_view = xT.rearrange("(c p j) n -> c p j n", p=P, j=J)
+        nc.sync.dma_start(out=w_raw[:], in_=w.rearrange("(c p j) m -> p c j m", p=P, j=J))
+        for c in range(PASSES - 1):
+            nc.sync.dma_start(out=x_raw[c][:], in_=x_view[c])
+        nc.sync.dma_start(out=x_half[0][:], in_=x_view[PASSES - 1][:, :, 0:H])
+        nc.sync.dma_start(out=offs_sb[:], in_=offs)
+        nc.sync.dma_start(out=b_sb[:], in_=b)
+        nc.sync.dma_start(out=x_half[1][:], in_=x_view[PASSES - 1][:, :, H:S])
+        nc.sync.dma_start(out=gate_sb[:], in_=gate)
+
+        nc.vector.memset(warm[:], 0.0)
+        nc.scalar.activation(out=warm[:], in_=warm[:], func=SILU)
+        nc.vector.memset(window[:], 0.0)
+
+        interleave(nc.vector.tensor_copy, w_grp[:, 0], w_raw[:, 0])
+        interleave(nc.scalar.copy, w_grp[:, 2], w_raw[:, 2])
+        interleave(nc.vector.tensor_copy, w_grp[:, 1], w_raw[:, 1])
+        for c in range(PASSES):
+            quantize(nc, w_codes[:, c], w_scales[:, c], w_grp[:, c])
+
+        def multiply(c, h):
+            cols = slice(h * H, (h + 1) * H)
+            nc.tensor.matmul_mx(
+                out=acc[h][:],
+                lhsT=w_codes[:, c].bitcast(FP8X4),
+                lhsT_scale=w_scales[:, c],
+                rhs=x_codes[c][:, cols].bitcast(FP8X4),
+                rhs_scale=x_scales[c][:, cols],
+                start=(c == 0),
+                stop=(c == PASSES - 1),
+            )
+
+        for c in range(PASSES - 1):
+            interleave(nc.vector.tensor_copy, x_grp[c][:, 0:H], x_raw[c][:, :, 0:H])
+            interleave(nc.scalar.copy, x_grp[c][:, H:S], x_raw[c][:, :, H:S])
+            for h in range(2):
+                cols = slice(h * H, (h + 1) * H)
+                quantize(nc, x_codes[c][:, cols], x_scales[c][:, cols], x_grp[c][:, cols])
+                multiply(c, h)
+
+        c = PASSES - 1
+        V = 160
+        for h in range(2):
+            cols = slice(h * H, (h + 1) * H)
+            interleave(nc.vector.tensor_copy, x_grp[c][:, h * H : h * H + V], x_half[h][:, :, 0:V])
+            interleave(nc.scalar.copy, x_grp[c][:, h * H + V : (h + 1) * H], x_half[h][:, :, V:H])
+            quantize(nc, x_codes[c][:, cols], x_scales[c][:, cols], x_grp[c][:, cols])
+            multiply(c, h)
+            nc.scalar.activation(out=y[:, cols], in_=acc[h][:], func=SILU, bias=b_sb[:])
+        for h in range(2):
+            cols = slice(h * H, (h + 1) * H)
+            places = offs_sb[:, h * H // 16 : (h + 1) * H // 16]
+            nc.vector.tensor_tensor(window[:].indirect(places), y[:, cols], gate_sb[:, cols], MULT)
+        nc.sync.dma_start(out=out, in_=window[:])

@@ -48,68 +48,68 @@ def tile_picked_place_lin_silu_srt_l_kernel(tc, xT, w, b, gate, offs, out):
         y = keep.tile([P, S], F32, name="y")
         warm = keep.tile([P, 1], F32, name="warm")
 
-        w_raw = keep.tile([P, PASSES, J, M], F32, name="w_raw")
-        w_grp = keep.tile([P, PASSES, M, J], BF16, name="w_grp", align_bytes=64)
-        w_codes = keep.tile([P, PASSES, M], U32, name="w_codes", align_bytes=64)
-        w_scales = keep.tile([P, PASSES, M], U8, name="w_scales", align_bytes=64)
-        x_raw = [keep.tile([P, J, S], F32, name=f"x_raw{c}") for c in range(PASSES - 1)]
-        x_half = [keep.tile([P, J, H], F32, name=f"x_half{h}") for h in range(2)]
+        w_raw = [keep.tile([P, J, M], F32, name=f"w_raw{c}") for c in range(PASSES)]
+        w_grp = [keep.tile([P, M, J], BF16, name=f"w_grp{c}", align_bytes=64) for c in range(PASSES)]
+        w_codes = [keep.tile([P, M], U32, name=f"w_codes{c}", align_bytes=64) for c in range(PASSES)]
+        w_scales = [keep.tile([P, M], U8, name=f"w_scales{c}", align_bytes=64) for c in range(PASSES)]
+        x_raw = [keep.tile([P, J, S], F32, name=f"x_raw{c}") for c in range(PASSES)]
         x_grp = [keep.tile([P, S, J], BF16, name=f"x_grp{c}", align_bytes=64) for c in range(PASSES)]
         x_codes = [keep.tile([P, S], U32, name=f"x_codes{c}", align_bytes=64) for c in range(PASSES)]
         x_scales = [keep.tile([P, S], U8, name=f"x_scales{c}", align_bytes=64) for c in range(PASSES)]
-        acc = [psum.tile([M, H], F32, name=f"acc{h}") for h in range(2)]
+        groups = [slice(0, 128), slice(128, 256), slice(256, 512)]
+        acc = [psum.tile([M, g.stop - g.start], F32, name=f"acc{i}") for i, g in enumerate(groups)]
 
         x_view = xT.rearrange("(c p j) n -> c p j n", p=P, j=J)
-        nc.sync.dma_start(out=w_raw[:], in_=w.rearrange("(c p j) m -> p c j m", p=P, j=J))
-        for c in range(PASSES - 1):
+        w_view = w.rearrange("(c p j) m -> c p j m", p=P, j=J)
+        nc.sync.dma_start(out=w_raw[0][:], in_=w_view[0])
+        for c in range(PASSES):
             nc.sync.dma_start(out=x_raw[c][:], in_=x_view[c])
-        nc.sync.dma_start(out=x_half[0][:], in_=x_view[PASSES - 1][:, :, 0:H])
-        nc.sync.dma_start(out=offs_sb[:], in_=offs)
+        nc.sync.dma_start(out=w_raw[1][:], in_=w_view[1])
+        nc.sync.dma_start(out=w_raw[2][:], in_=w_view[2])
         nc.sync.dma_start(out=b_sb[:], in_=b)
-        nc.sync.dma_start(out=x_half[1][:], in_=x_view[PASSES - 1][:, :, H:S])
         nc.sync.dma_start(out=gate_sb[:], in_=gate)
+        nc.sync.dma_start(out=offs_sb[:], in_=offs)
 
         nc.vector.memset(warm[:], 0.0)
         nc.scalar.activation(out=warm[:], in_=warm[:], func=SILU)
         nc.vector.memset(window[:], 0.0)
 
-        interleave(nc.vector.tensor_copy, w_grp[:, 0], w_raw[:, 0])
-        interleave(nc.scalar.copy, w_grp[:, 2], w_raw[:, 2])
-        interleave(nc.vector.tensor_copy, w_grp[:, 1], w_raw[:, 1])
+        def multiply(c):
+            for i, cols in enumerate(groups):
+                nc.tensor.matmul_mx(
+                    out=acc[i][:],
+                    lhsT=w_codes[c][:].bitcast(FP8X4),
+                    lhsT_scale=w_scales[c][:],
+                    rhs=x_codes[c][:, cols].bitcast(FP8X4),
+                    rhs_scale=x_scales[c][:, cols],
+                    start=(c == 0),
+                    stop=(c == PASSES - 1),
+                )
+
+        interleave(nc.vector.tensor_copy, w_grp[0][:, 0:80], w_raw[0][:, :, 0:80])
+        interleave(nc.scalar.copy, w_grp[0][:, 80:M], w_raw[0][:, :, 80:M])
+        quantize(nc, w_codes[0][:], w_scales[0][:], w_grp[0][:])
+
         for c in range(PASSES):
-            quantize(nc, w_codes[:, c], w_scales[:, c], w_grp[:, c])
-
-        def multiply(c, h):
-            cols = slice(h * H, (h + 1) * H)
-            nc.tensor.matmul_mx(
-                out=acc[h][:],
-                lhsT=w_codes[:, c].bitcast(FP8X4),
-                lhsT_scale=w_scales[:, c],
-                rhs=x_codes[c][:, cols].bitcast(FP8X4),
-                rhs_scale=x_scales[c][:, cols],
-                start=(c == 0),
-                stop=(c == PASSES - 1),
-            )
-
-        for c in range(PASSES - 1):
-            interleave(nc.vector.tensor_copy, x_grp[c][:, 0:H], x_raw[c][:, :, 0:H])
-            interleave(nc.scalar.copy, x_grp[c][:, H:S], x_raw[c][:, :, H:S])
+            V = 256 if c < 2 else 336
+            interleave(nc.vector.tensor_copy, x_grp[c][:, 0:V], x_raw[c][:, :, 0:V])
+            interleave(nc.scalar.copy, x_grp[c][:, V:S], x_raw[c][:, :, V:S])
             for h in range(2):
                 cols = slice(h * H, (h + 1) * H)
                 quantize(nc, x_codes[c][:, cols], x_scales[c][:, cols], x_grp[c][:, cols])
-                multiply(c, h)
+            if c == 0:
+                multiply(0)
 
-        c = PASSES - 1
-        V = 160
-        for h in range(2):
-            cols = slice(h * H, (h + 1) * H)
-            interleave(nc.vector.tensor_copy, x_grp[c][:, h * H : h * H + V], x_half[h][:, :, 0:V])
-            interleave(nc.scalar.copy, x_grp[c][:, h * H + V : (h + 1) * H], x_half[h][:, :, V:H])
-            quantize(nc, x_codes[c][:, cols], x_scales[c][:, cols], x_grp[c][:, cols])
-            multiply(c, h)
-            nc.scalar.activation(out=y[:, cols], in_=acc[h][:], func=SILU, bias=b_sb[:])
-        for h in range(2):
-            cols = slice(h * H, (h + 1) * H)
-            places = offs_sb[:, h * H // 16 : (h + 1) * H // 16]
+        interleave(nc.scalar.copy, w_grp[1][:], w_raw[1][:])
+        quantize(nc, w_codes[1][:], w_scales[1][:], w_grp[1][:])
+        multiply(1)
+        interleave(nc.vector.tensor_copy, w_grp[2][:, 0:96], w_raw[2][:, :, 0:96])
+        interleave(nc.scalar.copy, w_grp[2][:, 96:M], w_raw[2][:, :, 96:M])
+        quantize(nc, w_codes[2][:], w_scales[2][:], w_grp[2][:])
+        multiply(2)
+        for i, cols in enumerate(groups):
+            nc.scalar.activation(out=y[:, cols], in_=acc[i][:], func=SILU, bias=b_sb[:])
+        for cols in (slice(0, 128), slice(128, 512)):
+            places = offs_sb[:, cols.start // 16 : cols.stop // 16]
             nc.vector.tensor_tensor(window[:].indirect(places), y[:, cols], gate_sb[:, cols], MULT)
         nc.sync.dma_start(out=out, in_=window[:])

from contextlib import ExitStack

import concourse.mybir as mybir

K, S, M, T = 1536, 512, 128, 1024
FLOPS = 2 * K * S * M

F32 = mybir.dt.float32
BF16 = mybir.dt.bfloat16
U32 = mybir.dt.uint32
U16 = mybir.dt.uint16
U8 = mybir.dt.uint8
FP8X4 = mybir.dt.float8_e4m3fn_x4
SILU = mybir.ActivationFunctionType.Silu
MULT = mybir.AluOpType.mult

P = 128
J = 4
PASSES = K // (P * J)
H = S // 2


def interleave(copy, dst, src):
    copy(
        out=dst.rearrange("p (c i) j -> p c j i", i=4),
        in_=src.rearrange("p j (c i) -> p c j i", i=4),
    )


def quantize(nc, codes, scales, grouped):
    nc.vector.quantize_mx(
        out=codes.bitcast(FP8X4),
        scales=scales,
        in_=grouped.rearrange("p n j -> p (n j)"),
    )


def tile_picked_place_lin_silu_srt_l_kernel(tc, xT, w, b, gate, offs, out):
    nc = tc.nc
    with ExitStack() as ctx:
        keep = ctx.enter_context(tc.tile_pool(name="keep", bufs=1))
        psum = ctx.enter_context(tc.psum_pool(name="psum", bufs=1))

        offs_sb = keep.tile([P, S // 16], U16, name="offs_sb")
        b_sb = keep.tile([P, 1], F32, name="b_sb")
        gate_sb = keep.tile([P, S], F32, name="gate_sb")
        window = keep.tile([P, T], F32, name="window")
        y = keep.tile([P, S], F32, name="y")
        warm = keep.tile([P, 1], F32, name="warm")

        w_raw = [keep.tile([P, J, M], F32, name=f"w_raw{c}") for c in range(PASSES)]
        w_grp = [keep.tile([P, M, J], BF16, name=f"w_grp{c}", align_bytes=64) for c in range(PASSES)]
        w_codes = [keep.tile([P, M], U32, name=f"w_codes{c}", align_bytes=64) for c in range(PASSES)]
        w_scales = [keep.tile([P, M], U8, name=f"w_scales{c}", align_bytes=64) for c in range(PASSES)]
        x_raw = [keep.tile([P, J, S], F32, name=f"x_raw{c}") for c in range(PASSES)]
        x_grp = [keep.tile([P, S, J], BF16, name=f"x_grp{c}", align_bytes=64) for c in range(PASSES)]
        x_codes = [keep.tile([P, S], U32, name=f"x_codes{c}", align_bytes=64) for c in range(PASSES)]
        x_scales = [keep.tile([P, S], U8, name=f"x_scales{c}", align_bytes=64) for c in range(PASSES)]
        groups = [slice(0, 128), slice(128, 256), slice(256, 512)]
        acc = [psum.tile([M, g.stop - g.start], F32, name=f"acc{i}") for i, g in enumerate(groups)]

        x_view = xT.rearrange("(c p j) n -> c p j n", p=P, j=J)
        w_view = w.rearrange("(c p j) m -> c p j m", p=P, j=J)
        nc.sync.dma_start(out=w_raw[0][:], in_=w_view[0])
        for c in range(PASSES):
            nc.sync.dma_start(out=x_raw[c][:], in_=x_view[c])
        nc.sync.dma_start(out=w_raw[1][:], in_=w_view[1])
        nc.sync.dma_start(out=w_raw[2][:], in_=w_view[2])
        nc.sync.dma_start(out=b_sb[:], in_=b)
        nc.sync.dma_start(out=gate_sb[:], in_=gate)
        nc.sync.dma_start(out=offs_sb[:], in_=offs)

        nc.vector.memset(warm[:], 0.0)
        nc.scalar.activation(out=warm[:], in_=warm[:], func=SILU)
        nc.vector.memset(window[:], 0.0)

        def multiply(c):
            for i, cols in enumerate(groups):
                nc.tensor.matmul_mx(
                    out=acc[i][:],
                    lhsT=w_codes[c][:].bitcast(FP8X4),
                    lhsT_scale=w_scales[c][:],
                    rhs=x_codes[c][:, cols].bitcast(FP8X4),
                    rhs_scale=x_scales[c][:, cols],
                    start=(c == 0),
                    stop=(c == PASSES - 1),
                )

        interleave(nc.vector.tensor_copy, w_grp[0][:, 0:80], w_raw[0][:, :, 0:80])
        interleave(nc.scalar.copy, w_grp[0][:, 80:M], w_raw[0][:, :, 80:M])
        quantize(nc, w_codes[0][:], w_scales[0][:], w_grp[0][:])

        for c in range(PASSES):
            V = 256 if c < 2 else 336
            interleave(nc.vector.tensor_copy, x_grp[c][:, 0:V], x_raw[c][:, :, 0:V])
            interleave(nc.scalar.copy, x_grp[c][:, V:S], x_raw[c][:, :, V:S])
            for h in range(2):
                cols = slice(h * H, (h + 1) * H)
                quantize(nc, x_codes[c][:, cols], x_scales[c][:, cols], x_grp[c][:, cols])
            if c == 0:
                multiply(0)

        interleave(nc.scalar.copy, w_grp[1][:], w_raw[1][:])
        quantize(nc, w_codes[1][:], w_scales[1][:], w_grp[1][:])
        multiply(1)
        interleave(nc.vector.tensor_copy, w_grp[2][:, 0:96], w_raw[2][:, :, 0:96])
        interleave(nc.scalar.copy, w_grp[2][:, 96:M], w_raw[2][:, :, 96:M])
        quantize(nc, w_codes[2][:], w_scales[2][:], w_grp[2][:])
        multiply(2)
        for i, cols in enumerate(groups):
            nc.scalar.activation(out=y[:, cols], in_=acc[i][:], func=SILU, bias=b_sb[:])
        for cols in (slice(0, 128), slice(128, 512)):
            places = offs_sb[:, cols.start // 16 : cols.stop // 16]
            nc.vector.tensor_tensor(window[:].indirect(places), y[:, cols], gate_sb[:, cols], MULT)
        nc.sync.dma_start(out=out, in_=window[:])
